import numpy as np
import ml_dtypes


def mxq(x, axis, fmt="e4m3"):
    dtype, down = {"e4m3": (ml_dtypes.float8_e4m3fn, 7), "e5m2": (ml_dtypes.float8_e5m2, 14)}[fmt]
    v = np.moveaxis(np.asarray(x, np.float32).astype(ml_dtypes.bfloat16).astype(np.float64), axis, -1)
    blocks = v.reshape(v.shape[:-1] + (-1, 32))
    amax = np.abs(blocks).max(-1, keepdims=True)
    byte = np.maximum(np.where(amax > 0, np.frexp(amax)[1] - 1 + 127, 0) - down, 1)
    scale = np.exp2(byte - 127.0)
    codes = (blocks / scale).astype(np.float32).astype(dtype).astype(np.float64)
    return np.moveaxis((codes * scale).reshape(v.shape), -1, axis)


WIDE = False


def mx_kscale(k):
    if not WIDE:
        return np.ones(k)
    levels = np.array([10, -10, 5, -5, 0])
    if k % 512:
        return np.exp2(np.random.permutation(np.resize(levels, k // 32))).repeat(32)
    a = np.empty((k // 512, 16))
    for p in range(k // 512):
        a[p, :8] = np.random.permutation(np.resize(levels, 8))
        for g in range(8):
            far = levels[np.abs(levels - a[p, g]) >= 10]
            a[p, g + 8] = far[np.random.randint(len(far))]
    return np.exp2(a.ravel()).repeat(32)


def f64(x):
    return np.asarray(x).astype(np.float64)


def striped(idx):
    return np.tile(idx.reshape(-1, 16).T, (8, 1)).astype(np.uint16)


def unstriped(offs):
    return offs[:16].T.reshape(-1).astype(np.int64)


def striped8(idx):
    return np.concatenate([x.reshape(-1, 16).T for x in idx]).astype(np.uint16)


def runs(offs, k):
    lists = np.stack([offs[16 * r : 16 * r + 16].T.reshape(-1) for r in range(8)]).astype(np.int64)
    return lists[np.arange(k) % 512 // 64]


def pack_weight(w):
    k, n = w.shape
    w = f64(np.asarray(w, np.float32).astype(ml_dtypes.bfloat16)).reshape(k // 32, 32, n)
    amax = np.abs(w).max(1)
    byte = np.clip(np.where(amax > 0, np.frexp(amax)[1] - 1 + 127 - 7, 1), 1, 254)
    scaled = (w * np.exp2(127.0 - byte)[:, None, :]).reshape(k, n).astype(np.float32)
    words = np.ascontiguousarray(scaled.reshape(k // 512, 128, 4, n).transpose(0, 1, 3, 2)).astype(ml_dtypes.float8_e4m3fn).view(np.uint8)
    return words, np.ascontiguousarray(byte.astype(np.uint8).reshape(k // 512, 16, n))


def unpack_weight(words, scales):
    g, p, n, _ = words.shape
    vals = np.ascontiguousarray(words).view(ml_dtypes.float8_e4m3fn).astype(np.float64) * np.repeat(np.exp2(scales.astype(np.float64) - 127.0), 8, axis=1)[..., None]
    return vals.transpose(0, 1, 3, 2).reshape(g * 512, n)


E2M1 = np.array([0.0, 0.5, 1.0, 1.5, 2.0, 3.0, 4.0, 6.0, -0.0, -0.5, -1.0, -1.5, -2.0, -3.0, -4.0, -6.0])


def pack_fp4(w):
    k, n = w.shape
    w = f64(np.asarray(w, np.float32).astype(ml_dtypes.bfloat16)).reshape(k // 32, 32, n)
    amax = np.abs(w).max(1)
    mant, ex = np.frexp(amax / 6.0)
    byte = np.clip(np.where(amax > 0, np.where(mant > 0.5, ex, ex - 1) + 127, 1), 1, 254)
    scaled = (w * np.exp2(127.0 - byte)[:, None, :]).reshape(k, n).astype(np.float32)
    c = np.ascontiguousarray(scaled.reshape(k // 512, 128, 4, n).transpose(0, 1, 3, 2)).astype(ml_dtypes.float4_e2m1fn).view(np.uint8) & 0xF
    words = (c[..., 0::2] | (c[..., 1::2] << 4)).reshape(k // 512, 128, 2 * n)
    return np.ascontiguousarray(words), np.ascontiguousarray(byte.astype(np.uint8).reshape(k // 512, 16, n))


def unpack_fp4(words, scales):
    g, _, n = scales.shape
    words = np.ascontiguousarray(words).reshape(g, 128, n, 2)
    nib = np.empty((g, 128, n, 4), np.uint8)
    nib[..., 0::2] = words & 0xF
    nib[..., 1::2] = words >> 4
    vals = E2M1[nib] * np.repeat(np.exp2(scales.astype(np.float64) - 127.0), 8, axis=1)[..., None]
    return vals.transpose(0, 1, 3, 2).reshape(g * 512, n)


def sigmoid(v):
    return 1.0 / (1.0 + np.exp(-np.maximum(v, -700.0)))

def planes(y):
    n, m = y.shape
    v = y.astype(np.float32).astype(ml_dtypes.bfloat16).astype(np.float64).reshape(n // 32, 32, m)
    top = np.abs(v).max(1)
    byte = np.clip(np.where(top > 0, np.frexp(top)[1] - 1 + 127 - 7, 1), 1, 254)
    codes = (v * np.exp2(127.0 - byte)[:, None, :]).reshape(n, m).astype(np.float32).astype(ml_dtypes.float8_e4m3fn).view(np.uint8)
    words = codes.reshape(n // 512, 128, 4, m).transpose(0, 1, 3, 2)
    return np.ascontiguousarray(words), np.ascontiguousarray(byte.astype(np.uint8).reshape(n // 512, 16, m))


K, T, S, N, H, W, U = 512, 2048, 256, 512, 512, 1024, 1024


def setup_inputs():
    n = np.random.standard_normal
    s = mx_kscale(K)[:, None]
    u = mx_kscale(H)
    packed_xT = pack_weight(n((K, T)) * s)
    packed_w1 = pack_fp4(n((K, H)) / np.sqrt(K) / s)
    packed_w2 = pack_fp4(n((H, N)) / np.sqrt(H) / u[:, None])
    return {
        "x_words": packed_xT[0],
        "x_scales": packed_xT[1],
        "w1_words": packed_w1[0],
        "w1_scales": packed_w1[1],
        "gn": (np.random.uniform(0.5, 1.5, (H, 1)) * u[:, None]).astype(np.float32),
        "w2_words": packed_w2[0],
        "w2_scales": packed_w2[1],
        "mem": n((N, U)).astype(np.float32),
        "sl": np.random.uniform(1.0, 2.0, (N, 1)).astype(np.float32),
        "th": (0.5 * n((N, 1))).astype(np.float32),
        "offs": striped8(np.random.randint(0, T, (8, S))),
        "n1": striped(np.random.randint(0, S, W)),
        "n2": striped(np.random.permutation(U)[:S]),
        "n3": striped(np.random.permutation(S)),
    }


def reference(x_words, x_scales, w1_words, w1_scales, gn, w2_words, w2_scales, mem, sl, th, offs, n1, n2, n3):
    old = f64(mem)[:, unstriped(n2)]
    xq = unpack_weight(x_words, x_scales)[np.arange(K)[:, None], runs(offs, K)]
    y = unpack_fp4(w1_words, w1_scales).T @ xq
    mb = y[:, unstriped(n1)]
    ms = mb.reshape(H, S, 4).sum(axis=2)
    z = f64(gn) * (y * sigmoid(ms))
    h = unpack_fp4(w2_words, w2_scales).T @ mxq(z, 0, "e4m3")
    sg = sigmoid(f64(sl) * (h[:, unstriped(n3)] - f64(th)))
    nw = old + sg * (h - old)
    out = f64(mem).copy()
    out[:, unstriped(n2)] = nw
    return (out,) + planes(out)

@@ -1,0 +1,325 @@
+from contextlib import ExitStack
+
+import concourse.mybir as mybir
+
+K, T, S, N, H, U = 512, 2048, 256, 512, 512, 1024
+FLOPS = 2 * K * H * S + 2 * H * N * S
+
+F32 = mybir.dt.float32
+BF16 = mybir.dt.bfloat16
+I32 = mybir.dt.int32
+U32 = mybir.dt.uint32
+U16 = mybir.dt.uint16
+U8 = mybir.dt.uint8
+FP8X4 = mybir.dt.float8_e4m3fn_x4
+FP4X4 = mybir.dt.float4_e2m1fn_x4
+MULT = mybir.AluOpType.mult
+ADD = mybir.AluOpType.add
+SUB = mybir.AluOpType.subtract
+COPY = mybir.ActivationFunctionType.Copy
+SIGMOID = mybir.ActivationFunctionType.Sigmoid
+
+P = 128
+PACK = 4
+HALF = S // 2
+WIN = 520
+
+
+def tile_picked_hashgsumgepg_none_po_kernel(
+    tc, x_words, x_scales, w1_words, w1_scales, gn, w2_words, w2_scales, mem, sl, th,
+    offs, n1, n2, n3, out_0, out_1, out_2,
+):
+    nc = tc.nc
+    with ExitStack() as ctx:
+        lists = ctx.enter_context(tc.tile_pool(name="lists", bufs=1))
+        sb = ctx.enter_context(tc.tile_pool(name="sb", bufs=1))
+        psum = ctx.enter_context(tc.psum_pool(name="psum", bufs=1))
+
+        def new(shape, dtype, name, tag=None):
+            return sb.tile(shape, dtype, name=name, tag=tag or name, align_bytes=64)
+
+        offs_sb = lists.tile([P, S // 16], U16, name="offs_sb")
+        n1_sb = lists.tile([P, PACK * S // 16], U16, name="n1_sb")
+        n2_sb = lists.tile([P, S // 16], U16, name="n2_sb")
+        n3_sb = lists.tile([P, S // 16], U16, name="n3_sb")
+
+        xs_win = new([P, T], U8, "xs_win")
+        w1s_raw = new([P, H], U8, "w1s_raw")
+        w1w_raw = new([P, 2 * H], U8, "w1w_raw")
+        xw_win = new([P, T], U32, "xw_win")
+        nc.gpsimd.memset(xs_win[:].bitcast(I32), 0)
+        nc.vector.memset(w1s_raw[:].bitcast(I32), 0)
+        nc.sync.dma_start(offs_sb[:], offs)
+        nc.sync.dma_start(n1_sb[:], n1)
+        nc.sync.dma_start(n2_sb[:], n2)
+        nc.sync.dma_start(n3_sb[:], n3)
+        nc.sync.dma_start(w1w_raw[:].bitcast(I32), w1_words[0].bitcast(I32))
+        nc.sync.dma_start(xw_win[:].bitcast(I32), x_words[0].rearrange("p c t -> p (c t)").bitcast(I32))
+        w2w_raw = new([P, 2 * N], U8, "w2w_raw")
+        nc.sync.dma_start(w2w_raw[:].bitcast(I32), w2_words[0].bitcast(I32))
+        for e in range(2):
+            nc.scalar.dma_start(xs_win[:].bitcast(I32)[e:P:16, :], x_scales[0].bitcast(I32)[e:16:2, :])
+
+        def load_scale_rows(raw, scales, queues):
+            for q in range(4):
+                queues[q].dma_start(raw[:].bitcast(I32)[32 * q : 32 * q + 4, :], scales[0].bitcast(I32)[4 * q : 4 * q + 4, :])
+
+        def deal_words(dealt, raw):
+            nc.scalar.copy(dealt[:].bitcast(U16).rearrange("p (t m) -> p t m", t=PACK), raw[:].bitcast(U16).rearrange("p (m t) -> p t m", t=PACK))
+
+        def deal_scales(dealt, raw):
+            nc.vector.tensor_copy(dealt[:].rearrange("p (t m) -> p t m", t=PACK), raw[:].rearrange("p (m t) -> p t m", t=PACK))
+
+        load_scale_rows(w1s_raw, w1_scales, [nc.gpsimd, nc.gpsimd, nc.scalar, nc.scalar])
+
+        win = [new([P, WIN], F32, f"win{t}") for t in range(PACK)]
+        for t in range(PACK):
+            nc.vector.memset(win[t][:, S:], 0.0)
+
+        xs_got = new([P, S], U8, "xs_got")
+        nc.vector.tensor_copy(xs_got[:], xs_win[:].indirect(offs_sb[:]))
+        xs = new([P, S], U8, "xs")
+        nc.vector.tensor_copy(xs[:].bitcast(I32), xs_got[:].bitcast(I32))
+        for e in range(2):
+            nc.scalar.dma_start(xs[:].bitcast(I32)[2 + e : P : 32, :], xs_got[:].bitcast(I32)[16 + e : P : 32, :])
+        w1w = new([P, 2 * H], U8, "w1w")
+        deal_words(w1w, w1w_raw)
+        xq = new([P, S], U32, "xq")
+        nc.vector.tensor_copy(xq[:], xw_win[:].indirect(offs_sb[:]))
+        w1s = new([P, H], U8, "w1s")
+        deal_scales(w1s, w1s_raw)
+        w2w = new([P, 2 * N], U8, "w2w")
+        deal_words(w2w, w2w_raw)
+
+        rowvec = new([P, 3, 8], F32, "rowvec", "w1s_raw")
+        gn_sb, sl_sb, th_sb = (rowvec[:, i, :PACK] for i in range(3))
+        nc.sync.dma_start(gn_sb, gn.rearrange("(p t) o -> p (t o)", t=PACK))
+        w2s_raw = new([P, N], U8, "w2s_raw", "xs_got")
+        nc.gpsimd.memset(w2s_raw[:].bitcast(I32), 0)
+
+        y_ps = [psum.tile([P, S], F32, name=f"y_ps{t}") for t in range(PACK)]
+        for t in range(PACK):
+            nc.tensor.matmul_mx(
+                out=y_ps[t][:],
+                lhsT=w1w[:, 2 * P * t : 2 * P * (t + 1)].bitcast(FP4X4),
+                lhsT_scale=w1s[:, P * t : P * (t + 1)],
+                rhs=xq[:].bitcast(FP8X4),
+                rhs_scale=xs[:],
+                start=True,
+                stop=True,
+            )
+
+        mem_rows = mem.rearrange("(p t) u -> p t u", t=PACK)
+        out_rows = out_0.rearrange("(p t) u -> p t u", t=PACK)
+        page = [new([P, U], F32, f"page{t}", tag) for t, tag in enumerate(["xw_win", "xq", "w1w", "w1s"])]
+        load_scale_rows(w2s_raw, w2_scales, [nc.sync] * 4)
+        nc.sync.dma_start(sl_sb, sl.rearrange("(p t) o -> p (t o)", t=PACK))
+        nc.sync.dma_start(th_sb, th.rearrange("(p t) o -> p (t o)", t=PACK))
+        for t in range(PACK):
+            nc.sync.dma_start(page[t][:], mem_rows[:, t, :])
+
+        mb = {}
+        s2 = {}
+        ms = [new([P, PACK, HALF], F32, f"ms{h}") for h in range(2)]
+        sig = [new([P, PACK, HALF], F32, f"sig{h}") for h in range(2)]
+        zf = [new([P, PACK, HALF], F32, f"zf{h}") for h in range(2)]
+        zb = [new([P, HALF, PACK], BF16, f"zb{h}") for h in range(2)]
+        zq = [new([P, HALF], U32, f"zq{h}") for h in range(2)]
+        zs = [new([P, HALF], U8, f"zs{h}") for h in range(2)]
+        h_ps = [psum.tile([P, S], F32, name=f"h_ps{t}") for t in range(PACK)]
+
+        def leave_bank(bank, t, on_scalar):
+            if on_scalar:
+                nc.scalar.copy(win[t][:, :S], bank[:])
+            else:
+                nc.vector.tensor_copy(win[t][:, :S], bank[:])
+
+        def gather(dst, window, offsets, on_scalar):
+            if on_scalar:
+                nc.scalar.activation(dst, window.indirect(offsets), COPY)
+            else:
+                nc.vector.tensor_copy(dst, window.indirect(offsets))
+
+        def members(h, t, on_scalar):
+            mb[h, t] = new([P, HALF * PACK], F32, f"mb{h}{t}")
+            gather(mb[h, t][:], win[t][:], n1_sb[:, 32 * h : 32 * (h + 1)], on_scalar)
+
+        def members_shared(h, t):
+            mb[h, t] = new([P, HALF * PACK], F32, f"mb{h}{t}")
+            gather(mb[h, t][:, : 2 * HALF], win[t][:], n1_sb[:, 32 * h : 32 * h + 16], False)
+            gather(mb[h, t][:, 2 * HALF :], win[t][:], n1_sb[:, 32 * h + 16 : 32 * (h + 1)], True)
+
+        def sum_pairs(h, t):
+            s2[h, t] = new([P, HALF, 2], F32, f"s2{h}{t}")
+            quads = mb[h, t][:].rearrange("p (j a b) -> p j a b", a=2, b=2)
+            nc.vector.tensor_tensor(s2[h, t][:], quads[:, :, 0, :], quads[:, :, 1, :], ADD)
+
+        def sum_last(h, t):
+            nc.vector.tensor_tensor(ms[h][:, t, :], s2[h, t][:, :, 0], s2[h, t][:, :, 1], ADD)
+
+        def gate(h, t0, t1):
+            nc.scalar.activation(sig[h][:, t0:t1, :], ms[h][:, t0:t1, :], SIGMOID)
+
+        def make_z(h, t):
+            nc.vector.scalar_tensor_tensor(zf[h][:, t, :], y_ps[t][:, HALF * h : HALF * (h + 1)], gn_sb[:, t : t + 1], sig[h][:, t, :], MULT, MULT)
+
+        def second_product(h):
+            nc.vector.tensor_copy(zb[h][:], zf[h][:].rearrange("p t j -> p j t"))
+            nc.vector.quantize_mx(out=zq[h][:].bitcast(FP8X4), scales=zs[h][:], in_=zb[h][:].rearrange("p j t -> p (j t)"))
+            for t in range(PACK):
+                nc.tensor.matmul_mx(
+                    out=h_ps[t][:, HALF * h : HALF * (h + 1)],
+                    lhsT=w2w[:, 2 * P * t : 2 * P * (t + 1)].bitcast(FP4X4),
+                    lhsT_scale=w2s[:, P * t : P * (t + 1)],
+                    rhs=zq[h][:].bitcast(FP8X4),
+                    rhs_scale=zs[h][:],
+                    start=True,
+                    stop=True,
+                )
+
+        old = {}
+
+        def fetch_old(t, tag, on_scalar):
+            old[t] = new([P, S], F32, f"old{t}", tag)
+            gather(old[t][:], page[t][:], n2_sb[:], on_scalar)
+
+        leave_bank(y_ps[0], 0, True)
+        leave_bank(y_ps[1], 1, False)
+        members(0, 0, True)
+        members(0, 1, False)
+        leave_bank(y_ps[2], 2, True)
+        leave_bank(y_ps[3], 3, False)
+        members(0, 2, True)
+        sum_pairs(0, 0)
+        sum_pairs(0, 1)
+        sum_last(0, 0)
+        sum_last(0, 1)
+        members(0, 3, False)
+        members(1, 0, True)
+        members(1, 1, True)
+        sum_pairs(0, 2)
+        sum_pairs(0, 3)
+        sum_last(0, 2)
+        sum_last(0, 3)
+        gate(0, 0, 4)
+        members(1, 2, True)
+        w2s = new([P, N], U8, "w2s")
+        deal_scales(w2s, w2s_raw)
+        bias = new([P, PACK], F32, "bias")
+        nc.vector.scalar_tensor_tensor(bias[:], th_sb, -1.0, sl_sb, MULT, MULT)
+        sum_pairs(1, 0)
+        sum_pairs(1, 1)
+        sum_last(1, 0)
+        sum_last(1, 1)
+        for t in range(PACK):
+            make_z(0, t)
+        members_shared(1, 3)
+        gate(1, 0, 2)
+        second_product(0)
+        sum_pairs(1, 2)
+        make_z(1, 0)
+        sum_last(1, 2)
+        make_z(1, 1)
+        fetch_old(0, "mb12", True)
+        sum_pairs(1, 3)
+        sum_last(1, 3)
+        gate(1, 2, 4)
+        make_z(1, 2)
+        make_z(1, 3)
+        second_product(1)
+        fetch_old(1, "s213", True)
+        fetch_old(2, "ms1", True)
+        fetch_old(3, "zb1", False)
+
+        sg = [new([P, S], F32, f"sg{t}") for t in range(PACK)]
+        step = [new([P, S], F32, f"step{t}") for t in range(PACK)]
+        move = [new([P, S], F32, f"move{t}") for t in range(PACK)]
+        pairs = [new([P, 2, U // 2, 2], BF16, f"pairs{c}") for c in range(2)]
+        quads_out = [new([P, U // 4, PACK], BF16, f"quads_out{c}") for c in range(4)]
+        codes = new([P, U], U32, "codes")
+        bytes_out = new([P, U], U8, "bytes_out")
+
+        def write_gate(t):
+            nc.scalar.activation(sg[t][:], win[t][:].indirect(n3_sb[:]), SIGMOID, bias=bias[:, t : t + 1], scale=sl_sb[:, t : t + 1])
+
+        def diff(t):
+            nc.vector.tensor_tensor(step[t][:], h_ps[t][:], old[t][:], SUB)
+
+        def gated(t):
+            nc.vector.tensor_tensor(move[t][:], sg[t][:], step[t][:], MULT)
+
+        def put_on_vector(t):
+            nc.vector.tensor_tensor(page[t][:].indirect(n2_sb[:]), move[t][:], old[t][:], ADD)
+            nc.sync.dma_start(out_rows[:, t, :], page[t][:])
+
+        def add_old(t):
+            nc.vector.tensor_tensor(step[t][:], move[t][:], old[t][:], ADD)
+
+        def put_on_scalar(t):
+            nc.scalar.activation(page[t][:].indirect(n2_sb[:]), step[t][:], COPY)
+            nc.sync.dma_start(out_rows[:, t, :], page[t][:])
+
+        def round_page(t, c):
+            nc.vector.tensor_copy(pairs[c][:, t // 2, :, t % 2], page[t][:, U // 2 * c : U // 2 * (c + 1)])
+
+        def weave(c, on_scalar):
+            src = pairs[c // 2][:].rearrange("p a u b -> p (a u b)")
+            dst = quads_out[c][:].rearrange("p u t -> p (u t)")
+            cols = slice(U // 4 * (c % 2), U // 4 * (c % 2 + 1))
+            if on_scalar:
+                nc.scalar.copy(dst.bitcast(U32).rearrange("p (u a) -> p u a", a=2), src.bitcast(U32).rearrange("p (a u) -> p u a", a=2)[:, cols, :])
+            else:
+                nc.vector.tensor_copy(dst.bitcast(I32).rearrange("p (u a) -> p u a", a=2), src.bitcast(I32).rearrange("p (a u) -> p u a", a=2)[:, cols, :])
+
+        words_out = out_1[0].rearrange("p u t -> p (u t)").bitcast(I32)
+
+        def quantise_page(c):
+            cols = slice(U // 4 * c, U // 4 * (c + 1))
+            nc.vector.quantize_mx(out=codes[:, cols].bitcast(FP8X4), scales=bytes_out[:, cols], in_=quads_out[c][:].rearrange("p u t -> p (u t)"))
+
+        def store_words(c0, c1):
+            cols = slice(U // 4 * c0, U // 4 * c1)
+            nc.sync.dma_start(words_out[:, cols], codes[:].bitcast(I32)[:, cols])
+
+        leave_bank(h_ps[0], 0, True)
+        leave_bank(h_ps[1], 1, False)
+        write_gate(0)
+        write_gate(1)
+        diff(0)
+        diff(1)
+        leave_bank(h_ps[2], 2, True)
+        gated(0)
+        write_gate(2)
+        add_old(0)
+        gated(1)
+        put_on_scalar(0)
+        put_on_vector(1)
+        leave_bank(h_ps[3], 3, True)
+        write_gate(3)
+        diff(2)
+        diff(3)
+        gated(2)
+        round_page(1, 0)
+        add_old(2)
+        put_on_scalar(2)
+        gated(3)
+        round_page(1, 1)
+        add_old(3)
+        put_on_scalar(3)
+        for t in (0, 2, 3):
+            round_page(t, 0)
+            round_page(t, 1)
+        weave(0, True)
+        weave(1, True)
+        weave(2, False)
+        quantise_page(0)
+        weave(3, False)
+        quantise_page(1)
+        store_words(0, 2)
+        quantise_page(2)
+        quantise_page(3)
+        store_words(2, 4)
+
+        for q in range(4):
+            queue = nc.scalar if q % 2 == 0 else nc.sync
+            queue.dma_start(out_2[0].bitcast(I32)[4 * q : 4 * q + 4, :], bytes_out[:].bitcast(I32)[32 * q : 32 * q + 4, :])

@@ -72,6 +72,10 @@ def tile_picked_hashgsumgepg_none_po_kernel(
 
         load_scale_rows(w1s_raw, w1_scales, [nc.gpsimd, nc.gpsimd, nc.scalar, nc.scalar])
 
+        warm = new([P, 2, 8], F32, "warm")
+        nc.vector.memset(warm[:, 0, :1], 0.0)
+        nc.scalar.activation(warm[:, 1, :1], warm[:, 0, :1], SIGMOID)
+
         win = [new([P, WIN], F32, f"win{t}") for t in range(PACK)]
         for t in range(PACK):
             nc.vector.memset(win[t][:, S:], 0.0)

@@ -47,18 +47,18 @@ def tile_picked_hashgsumgepg_none_po_kernel(
         w1s_raw = new([P, H], U8, "w1s_raw")
         w1w_raw = new([P, 2 * H], U8, "w1w_raw")
         xw_win = new([P, T], U32, "xw_win")
-        nc.gpsimd.memset(xs_win[:].bitcast(I32), 0)
         nc.vector.memset(w1s_raw[:].bitcast(I32), 0)
+        nc.gpsimd.memset(xs_win[:].bitcast(I32), 0)
+        for e in range(2):
+            nc.sync.dma_start(xs_win[:].bitcast(I32)[e:P:16, :], x_scales[0].bitcast(I32)[e:16:2, :])
         nc.sync.dma_start(offs_sb[:], offs)
+        nc.sync.dma_start(w1w_raw[:].bitcast(I32), w1_words[0].bitcast(I32))
         nc.sync.dma_start(n1_sb[:], n1)
         nc.sync.dma_start(n2_sb[:], n2)
         nc.sync.dma_start(n3_sb[:], n3)
-        nc.sync.dma_start(w1w_raw[:].bitcast(I32), w1_words[0].bitcast(I32))
         nc.sync.dma_start(xw_win[:].bitcast(I32), x_words[0].rearrange("p c t -> p (c t)").bitcast(I32))
         w2w_raw = new([P, 2 * N], U8, "w2w_raw")
-        nc.sync.dma_start(w2w_raw[:].bitcast(I32), w2_words[0].bitcast(I32))
-        for e in range(2):
-            nc.scalar.dma_start(xs_win[:].bitcast(I32)[e:P:16, :], x_scales[0].bitcast(I32)[e:16:2, :])
+        nc.gpsimd.dma_start(w2w_raw[:].bitcast(I32), w2_words[0].bitcast(I32))
 
         def load_scale_rows(raw, scales, queues):
             for q in range(4):
@@ -70,7 +70,10 @@ def tile_picked_hashgsumgepg_none_po_kernel(
         def deal_scales(dealt, raw):
             nc.vector.tensor_copy(dealt[:].rearrange("p (t m) -> p t m", t=PACK), raw[:].rearrange("p (m t) -> p t m", t=PACK))
 
-        load_scale_rows(w1s_raw, w1_scales, [nc.gpsimd, nc.gpsimd, nc.scalar, nc.scalar])
+        load_scale_rows(w1s_raw, w1_scales, [nc.sync] * 4)
+        w2s_raw = new([P, N], U8, "w2s_raw")
+        nc.vector.memset(w2s_raw[:].bitcast(I32), 0)
+        load_scale_rows(w2s_raw, w2_scales, [nc.gpsimd] * 4)
 
         warm = new([P, 2, 8], F32, "warm")
         nc.vector.memset(warm[:, 0, :1], 0.0)
@@ -85,7 +88,7 @@ def tile_picked_hashgsumgepg_none_po_kernel(
         xs = new([P, S], U8, "xs")
         nc.vector.tensor_copy(xs[:].bitcast(I32), xs_got[:].bitcast(I32))
         for e in range(2):
-            nc.scalar.dma_start(xs[:].bitcast(I32)[2 + e : P : 32, :], xs_got[:].bitcast(I32)[16 + e : P : 32, :])
+            nc.sync.dma_start(xs[:].bitcast(I32)[2 + e : P : 32, :], xs_got[:].bitcast(I32)[16 + e : P : 32, :])
         w1w = new([P, 2 * H], U8, "w1w")
         deal_words(w1w, w1w_raw)
         xq = new([P, S], U32, "xq")
@@ -98,8 +101,6 @@ def tile_picked_hashgsumgepg_none_po_kernel(
         rowvec = new([P, 3, 8], F32, "rowvec", "w1s_raw")
         gn_sb, sl_sb, th_sb = (rowvec[:, i, :PACK] for i in range(3))
         nc.sync.dma_start(gn_sb, gn.rearrange("(p t) o -> p (t o)", t=PACK))
-        w2s_raw = new([P, N], U8, "w2s_raw", "xs_got")
-        nc.gpsimd.memset(w2s_raw[:].bitcast(I32), 0)
 
         y_ps = [psum.tile([P, S], F32, name=f"y_ps{t}") for t in range(PACK)]
         for t in range(PACK):
@@ -116,20 +117,20 @@ def tile_picked_hashgsumgepg_none_po_kernel(
         mem_rows = mem.rearrange("(p t) u -> p t u", t=PACK)
         out_rows = out_0.rearrange("(p t) u -> p t u", t=PACK)
         page = [new([P, U], F32, f"page{t}", tag) for t, tag in enumerate(["xw_win", "xq", "w1w", "w1s"])]
-        load_scale_rows(w2s_raw, w2_scales, [nc.sync] * 4)
         nc.sync.dma_start(sl_sb, sl.rearrange("(p t) o -> p (t o)", t=PACK))
         nc.sync.dma_start(th_sb, th.rearrange("(p t) o -> p (t o)", t=PACK))
         for t in range(PACK):
             nc.sync.dma_start(page[t][:], mem_rows[:, t, :])
 
-        mb = {}
-        s2 = {}
-        ms = [new([P, PACK, HALF], F32, f"ms{h}") for h in range(2)]
-        sig = [new([P, PACK, HALF], F32, f"sig{h}") for h in range(2)]
-        zf = [new([P, PACK, HALF], F32, f"zf{h}") for h in range(2)]
-        zb = [new([P, HALF, PACK], BF16, f"zb{h}") for h in range(2)]
-        zq = [new([P, HALF], U32, f"zq{h}") for h in range(2)]
-        zs = [new([P, HALF], U8, f"zs{h}") for h in range(2)]
+        mb = [new([P, S * PACK], F32, f"mb{t}") for t in range(PACK)]
+        pair_sums = new([P, PACK, S, 2], F32, "pair_sums")
+        ms = new([P, PACK - 1, S], F32, "ms")
+        ms_last = new([P, S], F32, "ms_last")
+        sig = new([P, PACK, S], F32, "sig")
+        zf = new([P, PACK, S], F32, "zf")
+        zb = new([P, S, PACK], BF16, "zb")
+        zq = new([P, S], U32, "zq")
+        zs = new([P, S], U8, "zs")
         h_ps = [psum.tile([P, S], F32, name=f"h_ps{t}") for t in range(PACK)]
 
         def leave_bank(bank, t, on_scalar):
@@ -144,96 +145,66 @@ def tile_picked_hashgsumgepg_none_po_kernel(
             else:
                 nc.vector.tensor_copy(dst, window.indirect(offsets))
 
-        def members(h, t, on_scalar):
-            mb[h, t] = new([P, HALF * PACK], F32, f"mb{h}{t}")
-            gather(mb[h, t][:], win[t][:], n1_sb[:, 32 * h : 32 * (h + 1)], on_scalar)
+        def members(t, c0, c1, on_scalar):
+            gather(mb[t][:, 16 * c0 : 16 * c1], win[t][:], n1_sb[:, c0:c1], on_scalar)
 
-        def members_shared(h, t):
-            mb[h, t] = new([P, HALF * PACK], F32, f"mb{h}{t}")
-            gather(mb[h, t][:, : 2 * HALF], win[t][:], n1_sb[:, 32 * h : 32 * h + 16], False)
-            gather(mb[h, t][:, 2 * HALF :], win[t][:], n1_sb[:, 32 * h + 16 : 32 * (h + 1)], True)
+        def sum_pairs(t, j0=0, j1=S):
+            quads = mb[t][:].rearrange("p (j a b) -> p j a b", a=2, b=2)
+            nc.vector.tensor_tensor(pair_sums[:, t, j0:j1, :], quads[:, j0:j1, 0, :], quads[:, j0:j1, 1, :], ADD)
 
-        def sum_pairs(h, t):
-            s2[h, t] = new([P, HALF, 2], F32, f"s2{h}{t}")
-            quads = mb[h, t][:].rearrange("p (j a b) -> p j a b", a=2, b=2)
-            nc.vector.tensor_tensor(s2[h, t][:], quads[:, :, 0, :], quads[:, :, 1, :], ADD)
+        def sum_last(dst, t0, t1):
+            nc.vector.tensor_tensor(dst, pair_sums[:, t0:t1, :, 0], pair_sums[:, t0:t1, :, 1], ADD)
 
-        def sum_last(h, t):
-            nc.vector.tensor_tensor(ms[h][:, t, :], s2[h, t][:, :, 0], s2[h, t][:, :, 1], ADD)
-
-        def gate(h, t0, t1):
-            nc.scalar.activation(sig[h][:, t0:t1, :], ms[h][:, t0:t1, :], SIGMOID)
-
-        def make_z(h, t):
-            nc.vector.scalar_tensor_tensor(zf[h][:, t, :], y_ps[t][:, HALF * h : HALF * (h + 1)], gn_sb[:, t : t + 1], sig[h][:, t, :], MULT, MULT)
-
-        def second_product(h):
-            nc.vector.tensor_copy(zb[h][:], zf[h][:].rearrange("p t j -> p j t"))
-            nc.vector.quantize_mx(out=zq[h][:].bitcast(FP8X4), scales=zs[h][:], in_=zb[h][:].rearrange("p j t -> p (j t)"))
-            for t in range(PACK):
-                nc.tensor.matmul_mx(
-                    out=h_ps[t][:, HALF * h : HALF * (h + 1)],
-                    lhsT=w2w[:, 2 * P * t : 2 * P * (t + 1)].bitcast(FP4X4),
-                    lhsT_scale=w2s[:, P * t : P * (t + 1)],
-                    rhs=zq[h][:].bitcast(FP8X4),
-                    rhs_scale=zs[h][:],
-                    start=True,
-                    stop=True,
-                )
-
-        old = {}
-
-        def fetch_old(t, tag, on_scalar):
-            old[t] = new([P, S], F32, f"old{t}", tag)
-            gather(old[t][:], page[t][:], n2_sb[:], on_scalar)
+        def make_z(t):
+            nc.vector.scalar_tensor_tensor(zf[:, t, :], y_ps[t][:], gn_sb[:, t : t + 1], sig[:, t, :], MULT, MULT)
 
         leave_bank(y_ps[0], 0, True)
         leave_bank(y_ps[1], 1, False)
-        members(0, 0, True)
-        members(0, 1, False)
+        members(0, 0, 32, True)
+        members(1, 0, 32, False)
         leave_bank(y_ps[2], 2, True)
         leave_bank(y_ps[3], 3, False)
-        members(0, 2, True)
-        sum_pairs(0, 0)
-        sum_pairs(0, 1)
-        sum_last(0, 0)
-        sum_last(0, 1)
-        members(0, 3, False)
-        members(1, 0, True)
-        members(1, 1, True)
-        sum_pairs(0, 2)
-        sum_pairs(0, 3)
-        sum_last(0, 2)
-        sum_last(0, 3)
-        gate(0, 0, 4)
-        members(1, 2, True)
-        w2s = new([P, N], U8, "w2s")
+        members(0, 32, 64, True)
+        members(1, 32, 64, False)
+        members(2, 0, 32, True)
+        members(3, 0, 16, False)
+        members(2, 32, 64, True)
+        members(3, 16, 40, True)
+        members(3, 40, 64, True)
+        sum_pairs(0)
+        sum_pairs(1)
+        sum_last(ms[:, 0:2, :], 0, 2)
+        sum_pairs(2)
+        w2s = new([P, N], U8, "w2s", "xs")
         deal_scales(w2s, w2s_raw)
         bias = new([P, PACK], F32, "bias")
         nc.vector.scalar_tensor_tensor(bias[:], th_sb, -1.0, sl_sb, MULT, MULT)
-        sum_pairs(1, 0)
-        sum_pairs(1, 1)
-        sum_last(1, 0)
-        sum_last(1, 1)
+        sum_last(ms[:, 2:3, :], 2, 3)
+        sum_pairs(3, 0, 160)
+        sum_pairs(3, 160, S)
+        sum_last(ms_last[:].unsqueeze(1), 3, 4)
+        nc.scalar.activation(sig[:, 0:2, :], ms[:, 0:2, :], SIGMOID)
+        nc.scalar.activation(sig[:, 2, :], ms[:, 2, :], SIGMOID)
+        nc.scalar.activation(sig[:, 3, :], ms_last[:], SIGMOID)
         for t in range(PACK):
-            make_z(0, t)
-        members_shared(1, 3)
-        gate(1, 0, 2)
-        second_product(0)
-        sum_pairs(1, 2)
-        make_z(1, 0)
-        sum_last(1, 2)
-        make_z(1, 1)
-        fetch_old(0, "mb12", True)
-        sum_pairs(1, 3)
-        sum_last(1, 3)
-        gate(1, 2, 4)
-        make_z(1, 2)
-        make_z(1, 3)
-        second_product(1)
-        fetch_old(1, "s213", True)
-        fetch_old(2, "ms1", True)
-        fetch_old(3, "zb1", False)
+            make_z(t)
+        nc.vector.tensor_copy(zb[:], zf[:].rearrange("p t j -> p j t"))
+        nc.vector.quantize_mx(out=zq[:].bitcast(FP8X4), scales=zs[:], in_=zb[:].rearrange("p j t -> p (j t)"))
+        for t in range(PACK):
+            nc.tensor.matmul_mx(
+                out=h_ps[t][:],
+                lhsT=w2w[:, 2 * P * t : 2 * P * (t + 1)].bitcast(FP4X4),
+                lhsT_scale=w2s[:, P * t : P * (t + 1)],
+                rhs=zq[:].bitcast(FP8X4),
+                rhs_scale=zs[:],
+                start=True,
+                stop=True,
+            )
+        old_first = new([P, PACK - 1, S], F32, "old_first", "ms_last")
+        old_last = new([P, S], F32, "old_last", "zb")
+        old = [old_first[:, t, :] for t in range(PACK - 1)] + [old_last[:]]
+        for t in range(PACK):
+            gather(old[t], page[t][:], n2_sb[:], t < PACK - 1)
 
         sg = [new([P, S], F32, f"sg{t}") for t in range(PACK)]
         step = [new([P, S], F32, f"step{t}") for t in range(PACK)]
@@ -247,17 +218,17 @@ def tile_picked_hashgsumgepg_none_po_kernel(
             nc.scalar.activation(sg[t][:], win[t][:].indirect(n3_sb[:]), SIGMOID, bias=bias[:, t : t + 1], scale=sl_sb[:, t : t + 1])
 
         def diff(t):
-            nc.vector.tensor_tensor(step[t][:], h_ps[t][:], old[t][:], SUB)
+            nc.vector.tensor_tensor(step[t][:], h_ps[t][:], old[t], SUB)
 
         def gated(t):
             nc.vector.tensor_tensor(move[t][:], sg[t][:], step[t][:], MULT)
 
         def put_on_vector(t):
-            nc.vector.tensor_tensor(page[t][:].indirect(n2_sb[:]), move[t][:], old[t][:], ADD)
+            nc.vector.tensor_tensor(page[t][:].indirect(n2_sb[:]), move[t][:], old[t], ADD)
             nc.sync.dma_start(out_rows[:, t, :], page[t][:])
 
         def add_old(t):
-            nc.vector.tensor_tensor(step[t][:], move[t][:], old[t][:], ADD)
+            nc.vector.tensor_tensor(step[t][:], move[t][:], old[t], ADD)
 
         def put_on_scalar(t):
             nc.scalar.activation(page[t][:].indirect(n2_sb[:]), step[t][:], COPY)
@@ -286,43 +257,39 @@ def tile_picked_hashgsumgepg_none_po_kernel(
             nc.sync.dma_start(words_out[:, cols], codes[:].bitcast(I32)[:, cols])
 
         leave_bank(h_ps[0], 0, True)
-        leave_bank(h_ps[1], 1, False)
-        write_gate(0)
-        write_gate(1)
+        leave_bank(h_ps[1], 1, True)
+        leave_bank(h_ps[2], 2, False)
+        leave_bank(h_ps[3], 3, False)
+        for t in range(PACK):
+            write_gate(t)
         diff(0)
-        diff(1)
-        leave_bank(h_ps[2], 2, True)
         gated(0)
-        write_gate(2)
+        diff(1)
         add_old(0)
-        gated(1)
         put_on_scalar(0)
-        put_on_vector(1)
-        leave_bank(h_ps[3], 3, True)
-        write_gate(3)
         diff(2)
-        diff(3)
+        gated(1)
         gated(2)
-        round_page(1, 0)
+        diff(3)
         add_old(2)
         put_on_scalar(2)
         gated(3)
-        round_page(1, 1)
         add_old(3)
         put_on_scalar(3)
-        for t in (0, 2, 3):
+        put_on_vector(1)
+        for t in (0, 2, 1, 3):
             round_page(t, 0)
             round_page(t, 1)
         weave(0, True)
         weave(1, True)
         weave(2, False)
+        weave(3, True)
         quantise_page(0)
-        weave(3, False)
-        quantise_page(1)
-        store_words(0, 2)
         quantise_page(2)
+        quantise_page(1)
+        store_words(0, 3)
         quantise_page(3)
-        store_words(2, 4)
+        store_words(3, 4)
 
         for q in range(4):
             queue = nc.scalar if q % 2 == 0 else nc.sync

@@ -1,6 +1,7 @@
 from contextlib import ExitStack
 
 import concourse.mybir as mybir
+from concourse.masks import make_identity
 
 K, T, S, N, H, U = 512, 2048, 256, 512, 512, 1024
 FLOPS = 2 * K * H * S + 2 * H * N * S
@@ -57,6 +58,8 @@ def tile_picked_hashgsumgepg_none_po_kernel(
         nc.sync.dma_start(n2_sb[:], n2)
         nc.sync.dma_start(n3_sb[:], n3)
         nc.sync.dma_start(xw_win[:].bitcast(I32), x_words[0].rearrange("p c t -> p (c t)").bitcast(I32))
+        ident = new([P, P], F32, "ident")
+        make_identity(nc, ident[:])
         w2w_raw = new([P, 2 * N], U8, "w2w_raw")
         nc.gpsimd.dma_start(w2w_raw[:].bitcast(I32), w2_words[0].bitcast(I32))
 
@@ -123,10 +126,11 @@ def tile_picked_hashgsumgepg_none_po_kernel(
             nc.sync.dma_start(page[t][:], mem_rows[:, t, :])
 
         mb = [new([P, S * PACK], F32, f"mb{t}") for t in range(PACK)]
-        pair_sums = new([P, PACK, S, 2], F32, "pair_sums")
-        ms = new([P, PACK - 1, S], F32, "ms")
+        pair_sums = new([P, 2, S, 2], F32, "pair_sums")
+        ms = new([P, S], F32, "ms")
         ms_last = new([P, S], F32, "ms_last")
-        sig = new([P, PACK, S], F32, "sig")
+        sig = new([P, 2, S], F32, "sig")
+        sig_turned = new([P, PACK, P], F32, "sig_turned")
         zf = new([P, PACK, S], F32, "zf")
         zb = new([P, S, PACK], BF16, "zb")
         zq = new([P, S], U32, "zq")
@@ -150,13 +154,17 @@ def tile_picked_hashgsumgepg_none_po_kernel(
 
         def sum_pairs(t, j0=0, j1=S):
             quads = mb[t][:].rearrange("p (j a b) -> p j a b", a=2, b=2)
-            nc.vector.tensor_tensor(pair_sums[:, t, j0:j1, :], quads[:, j0:j1, 0, :], quads[:, j0:j1, 1, :], ADD)
+            nc.vector.tensor_tensor(pair_sums[:, t - 2, j0:j1, :], quads[:, j0:j1, 0, :], quads[:, j0:j1, 1, :], ADD)
 
-        def sum_last(dst, t0, t1):
-            nc.vector.tensor_tensor(dst, pair_sums[:, t0:t1, :, 0], pair_sums[:, t0:t1, :, 1], ADD)
+        def sum_last(dst, t):
+            nc.vector.tensor_tensor(dst[:], pair_sums[:, t - 2, :, 0], pair_sums[:, t - 2, :, 1], ADD)
 
-        def make_z(t):
-            nc.vector.scalar_tensor_tensor(zf[:, t, :], y_ps[t][:], gn_sb[:, t : t + 1], sig[:, t, :], MULT, MULT)
+        def sum_turned(t, c):
+            for m in range(PACK):
+                nc.tensor.matmul(ms_turned[:, 2 * t + c, :], mb[t][:, PACK * P * c + m : PACK * P * (c + 1) : PACK], ident[:], start=m == 0, stop=m == PACK - 1, is_transpose=True)
+
+        def make_z(t, y, gates):
+            nc.vector.scalar_tensor_tensor(zf[:, t, :], y, gn_sb[:, t : t + 1], gates, MULT, MULT)
 
         leave_bank(y_ps[0], 0, True)
         leave_bank(y_ps[1], 1, False)
@@ -166,28 +174,35 @@ def tile_picked_hashgsumgepg_none_po_kernel(
         leave_bank(y_ps[3], 3, False)
         members(0, 32, 64, True)
         members(1, 32, 64, False)
+        ms_turned = psum.tile([P, PACK, P], F32, name="ms_turned", tag="y_ps0")
+        for c in range(2):
+            for t in range(2):
+                sum_turned(t, c)
         members(2, 0, 32, True)
-        members(3, 0, 16, False)
+        members(3, 0, 32, False)
         members(2, 32, 64, True)
-        members(3, 16, 40, True)
-        members(3, 40, 64, True)
-        sum_pairs(0)
-        sum_pairs(1)
-        sum_last(ms[:, 0:2, :], 0, 2)
-        sum_pairs(2)
+        members(3, 32, 42, False)
+        members(3, 42, 64, True)
+        sum_pairs(3, 0, 168)
         w2s = new([P, N], U8, "w2s", "xs")
         deal_scales(w2s, w2s_raw)
         bias = new([P, PACK], F32, "bias")
         nc.vector.scalar_tensor_tensor(bias[:], th_sb, -1.0, sl_sb, MULT, MULT)
-        sum_last(ms[:, 2:3, :], 2, 3)
-        sum_pairs(3, 0, 160)
-        sum_pairs(3, 160, S)
-        sum_last(ms_last[:].unsqueeze(1), 3, 4)
-        nc.scalar.activation(sig[:, 0:2, :], ms[:, 0:2, :], SIGMOID)
-        nc.scalar.activation(sig[:, 2, :], ms[:, 2, :], SIGMOID)
-        nc.scalar.activation(sig[:, 3, :], ms_last[:], SIGMOID)
-        for t in range(PACK):
-            make_z(t)
+        sum_pairs(2)
+        sum_pairs(3, 168, S)
+        sum_last(ms, 2)
+        sum_last(ms_last, 3)
+        nc.scalar.activation(sig_turned[:], ms_turned[:], SIGMOID)
+        sig_back = psum.tile([P, 2, S], F32, name="sig_back", tag="y_ps1")
+        for t in range(2):
+            for c in range(2):
+                nc.tensor.transpose(sig_back[:, t, P * c : P * (c + 1)], sig_turned[:, 2 * t + c, :], ident[:])
+        nc.scalar.activation(sig[:, 0, :], ms[:], SIGMOID)
+        nc.scalar.activation(sig[:, 1, :], ms_last[:], SIGMOID)
+        for t in range(2):
+            make_z(t, win[t][:, :S], sig_back[:, t, :])
+        for t in range(2, PACK):
+            make_z(t, y_ps[t][:], sig[:, t - 2, :])
         nc.vector.tensor_copy(zb[:], zf[:].rearrange("p t j -> p j t"))
         nc.vector.quantize_mx(out=zq[:].bitcast(FP8X4), scales=zs[:], in_=zb[:].rearrange("p j t -> p (j t)"))
         for t in range(PACK):

from contextlib import ExitStack

import concourse.mybir as mybir
from concourse.masks import make_identity

K, T, S, N, H, U = 512, 2048, 256, 512, 512, 1024
FLOPS = 2 * K * H * S + 2 * H * N * S

F32 = mybir.dt.float32
BF16 = mybir.dt.bfloat16
I32 = mybir.dt.int32
U32 = mybir.dt.uint32
U16 = mybir.dt.uint16
U8 = mybir.dt.uint8
FP8X4 = mybir.dt.float8_e4m3fn_x4
FP4X4 = mybir.dt.float4_e2m1fn_x4
MULT = mybir.AluOpType.mult
ADD = mybir.AluOpType.add
SUB = mybir.AluOpType.subtract
COPY = mybir.ActivationFunctionType.Copy
SIGMOID = mybir.ActivationFunctionType.Sigmoid

P = 128
PACK = 4
HALF = S // 2
WIN = 520


def tile_picked_hashgsumgepg_none_po_kernel(
    tc, x_words, x_scales, w1_words, w1_scales, gn, w2_words, w2_scales, mem, sl, th,
    offs, n1, n2, n3, out_0, out_1, out_2,
):
    nc = tc.nc
    with ExitStack() as ctx:
        lists = ctx.enter_context(tc.tile_pool(name="lists", bufs=1))
        sb = ctx.enter_context(tc.tile_pool(name="sb", bufs=1))
        psum = ctx.enter_context(tc.psum_pool(name="psum", bufs=1))

        def new(shape, dtype, name, tag=None):
            return sb.tile(shape, dtype, name=name, tag=tag or name, align_bytes=64)

        offs_sb = lists.tile([P, S // 16], U16, name="offs_sb")
        n1_sb = lists.tile([P, PACK * S // 16], U16, name="n1_sb")
        n2_sb = lists.tile([P, S // 16], U16, name="n2_sb")
        n3_sb = lists.tile([P, S // 16], U16, name="n3_sb")

        xs_win = new([P, T], U8, "xs_win")
        w1s_raw = new([P, H], U8, "w1s_raw")
        w1w_raw = new([P, 2 * H], U8, "w1w_raw")
        xw_win = new([P, T], U32, "xw_win")
        nc.vector.memset(w1s_raw[:].bitcast(I32), 0)
        nc.gpsimd.memset(xs_win[:].bitcast(I32), 0)
        for e in range(2):
            nc.sync.dma_start(xs_win[:].bitcast(I32)[e:P:16, :], x_scales[0].bitcast(I32)[e:16:2, :])
        nc.sync.dma_start(offs_sb[:], offs)
        nc.sync.dma_start(w1w_raw[:].bitcast(I32), w1_words[0].bitcast(I32))
        nc.sync.dma_start(n1_sb[:], n1)
        nc.sync.dma_start(n2_sb[:], n2)
        nc.sync.dma_start(n3_sb[:], n3)
        nc.sync.dma_start(xw_win[:].bitcast(I32), x_words[0].rearrange("p c t -> p (c t)").bitcast(I32))
        ident = new([P, P], F32, "ident")
        make_identity(nc, ident[:])
        w2w_raw = new([P, 2 * N], U8, "w2w_raw")
        nc.gpsimd.dma_start(w2w_raw[:].bitcast(I32), w2_words[0].bitcast(I32))

        def load_scale_rows(raw, scales, queues):
            for q in range(4):
                queues[q].dma_start(raw[:].bitcast(I32)[32 * q : 32 * q + 4, :], scales[0].bitcast(I32)[4 * q : 4 * q + 4, :])

        def deal_words(dealt, raw):
            nc.scalar.copy(dealt[:].bitcast(U16).rearrange("p (t m) -> p t m", t=PACK), raw[:].bitcast(U16).rearrange("p (m t) -> p t m", t=PACK))

        def deal_scales(dealt, raw):
            nc.vector.tensor_copy(dealt[:].rearrange("p (t m) -> p t m", t=PACK), raw[:].rearrange("p (m t) -> p t m", t=PACK))

        load_scale_rows(w1s_raw, w1_scales, [nc.sync] * 4)
        w2s_raw = new([P, N], U8, "w2s_raw")
        nc.vector.memset(w2s_raw[:].bitcast(I32), 0)
        load_scale_rows(w2s_raw, w2_scales, [nc.gpsimd] * 4)

        warm = new([P, 2, 8], F32, "warm")
        nc.vector.memset(warm[:, 0, :1], 0.0)
        nc.scalar.activation(warm[:, 1, :1], warm[:, 0, :1], SIGMOID)

        win = [new([P, WIN], F32, f"win{t}") for t in range(PACK)]
        for t in range(PACK):
            nc.vector.memset(win[t][:, S:], 0.0)

        xs_got = new([P, S], U8, "xs_got")
        nc.vector.tensor_copy(xs_got[:], xs_win[:].indirect(offs_sb[:]))
        xs = new([P, S], U8, "xs")
        nc.vector.tensor_copy(xs[:].bitcast(I32), xs_got[:].bitcast(I32))
        for e in range(2):
            nc.sync.dma_start(xs[:].bitcast(I32)[2 + e : P : 32, :], xs_got[:].bitcast(I32)[16 + e : P : 32, :])
        w1w = new([P, 2 * H], U8, "w1w")
        deal_words(w1w, w1w_raw)
        xq = new([P, S], U32, "xq")
        nc.vector.tensor_copy(xq[:], xw_win[:].indirect(offs_sb[:]))
        w1s = new([P, H], U8, "w1s")
        deal_scales(w1s, w1s_raw)
        w2w = new([P, 2 * N], U8, "w2w")
        deal_words(w2w, w2w_raw)

        rowvec = new([P, 3, 8], F32, "rowvec", "w1s_raw")
        gn_sb, sl_sb, th_sb = (rowvec[:, i, :PACK] for i in range(3))
        nc.sync.dma_start(gn_sb, gn.rearrange("(p t) o -> p (t o)", t=PACK))

        y_ps = [psum.tile([P, S], F32, name=f"y_ps{t}") for t in range(PACK)]
        for t in range(PACK):
            nc.tensor.matmul_mx(
                out=y_ps[t][:],
                lhsT=w1w[:, 2 * P * t : 2 * P * (t + 1)].bitcast(FP4X4),
                lhsT_scale=w1s[:, P * t : P * (t + 1)],
                rhs=xq[:].bitcast(FP8X4),
                rhs_scale=xs[:],
                start=True,
                stop=True,
            )

        mem_rows = mem.rearrange("(p t) u -> p t u", t=PACK)
        out_rows = out_0.rearrange("(p t) u -> p t u", t=PACK)
        page = [new([P, U], F32, f"page{t}", tag) for t, tag in enumerate(["xw_win", "xq", "w1w", "w1s"])]
        nc.sync.dma_start(sl_sb, sl.rearrange("(p t) o -> p (t o)", t=PACK))
        nc.sync.dma_start(th_sb, th.rearrange("(p t) o -> p (t o)", t=PACK))
        for t in range(PACK):
            nc.sync.dma_start(page[t][:], mem_rows[:, t, :])

        mb = [new([P, S * PACK], F32, f"mb{t}") for t in range(PACK)]
        pair_sums = new([P, 2, S, 2], F32, "pair_sums")
        ms = new([P, S], F32, "ms")
        ms_last = new([P, S], F32, "ms_last")
        sig = new([P, 2, S], F32, "sig")
        sig_turned = new([P, PACK, P], F32, "sig_turned")
        zf = new([P, PACK, S], F32, "zf")
        zb = new([P, S, PACK], BF16, "zb")
        zq = new([P, S], U32, "zq")
        zs = new([P, S], U8, "zs")
        h_ps = [psum.tile([P, S], F32, name=f"h_ps{t}") for t in range(PACK)]

        def leave_bank(bank, t, on_scalar):
            if on_scalar:
                nc.scalar.copy(win[t][:, :S], bank[:])
            else:
                nc.vector.tensor_copy(win[t][:, :S], bank[:])

        def gather(dst, window, offsets, on_scalar):
            if on_scalar:
                nc.scalar.activation(dst, window.indirect(offsets), COPY)
            else:
                nc.vector.tensor_copy(dst, window.indirect(offsets))

        def members(t, c0, c1, on_scalar):
            gather(mb[t][:, 16 * c0 : 16 * c1], win[t][:], n1_sb[:, c0:c1], on_scalar)

        def sum_pairs(t, j0=0, j1=S):
            quads = mb[t][:].rearrange("p (j a b) -> p j a b", a=2, b=2)
            nc.vector.tensor_tensor(pair_sums[:, t - 2, j0:j1, :], quads[:, j0:j1, 0, :], quads[:, j0:j1, 1, :], ADD)

        def sum_last(dst, t):
            nc.vector.tensor_tensor(dst[:], pair_sums[:, t - 2, :, 0], pair_sums[:, t - 2, :, 1], ADD)

        def sum_turned(t, c):
            for m in range(PACK):
                nc.tensor.matmul(ms_turned[:, 2 * t + c, :], mb[t][:, PACK * P * c + m : PACK * P * (c + 1) : PACK], ident[:], start=m == 0, stop=m == PACK - 1, is_transpose=True)

        def make_z(t, y, gates):
            nc.vector.scalar_tensor_tensor(zf[:, t, :], y, gn_sb[:, t : t + 1], gates, MULT, MULT)

        leave_bank(y_ps[0], 0, True)
        leave_bank(y_ps[1], 1, False)
        members(0, 0, 32, True)
        members(1, 0, 32, False)
        leave_bank(y_ps[2], 2, True)
        leave_bank(y_ps[3], 3, False)
        members(0, 32, 64, True)
        members(1, 32, 64, False)
        ms_turned = psum.tile([P, PACK, P], F32, name="ms_turned", tag="y_ps0")
        for c in range(2):
            for t in range(2):
                sum_turned(t, c)
        members(2, 0, 32, True)
        members(3, 0, 32, False)
        members(2, 32, 64, True)
        members(3, 32, 42, False)
        members(3, 42, 64, True)
        sum_pairs(3, 0, 168)
        w2s = new([P, N], U8, "w2s", "xs")
        deal_scales(w2s, w2s_raw)
        bias = new([P, PACK], F32, "bias")
        nc.vector.scalar_tensor_tensor(bias[:], th_sb, -1.0, sl_sb, MULT, MULT)
        sum_pairs(2)
        sum_pairs(3, 168, S)
        sum_last(ms, 2)
        sum_last(ms_last, 3)
        nc.scalar.activation(sig_turned[:], ms_turned[:], SIGMOID)
        sig_back = psum.tile([P, 2, S], F32, name="sig_back", tag="y_ps1")
        for t in range(2):
            for c in range(2):
                nc.tensor.transpose(sig_back[:, t, P * c : P * (c + 1)], sig_turned[:, 2 * t + c, :], ident[:])
        nc.scalar.activation(sig[:, 0, :], ms[:], SIGMOID)
        nc.scalar.activation(sig[:, 1, :], ms_last[:], SIGMOID)
        for t in range(2):
            make_z(t, win[t][:, :S], sig_back[:, t, :])
        for t in range(2, PACK):
            make_z(t, y_ps[t][:], sig[:, t - 2, :])
        nc.vector.tensor_copy(zb[:], zf[:].rearrange("p t j -> p j t"))
        nc.vector.quantize_mx(out=zq[:].bitcast(FP8X4), scales=zs[:], in_=zb[:].rearrange("p j t -> p (j t)"))
        for t in range(PACK):
            nc.tensor.matmul_mx(
                out=h_ps[t][:],
                lhsT=w2w[:, 2 * P * t : 2 * P * (t + 1)].bitcast(FP4X4),
                lhsT_scale=w2s[:, P * t : P * (t + 1)],
                rhs=zq[:].bitcast(FP8X4),
                rhs_scale=zs[:],
                start=True,
                stop=True,
            )
        old_first = new([P, PACK - 1, S], F32, "old_first", "ms_last")
        old_last = new([P, S], F32, "old_last", "zb")
        old = [old_first[:, t, :] for t in range(PACK - 1)] + [old_last[:]]
        for t in range(PACK):
            gather(old[t], page[t][:], n2_sb[:], t < PACK - 1)

        sg = [new([P, S], F32, f"sg{t}") for t in range(PACK)]
        step = [new([P, S], F32, f"step{t}") for t in range(PACK)]
        move = [new([P, S], F32, f"move{t}") for t in range(PACK)]
        pairs = [new([P, 2, U // 2, 2], BF16, f"pairs{c}") for c in range(2)]
        quads_out = [new([P, U // 4, PACK], BF16, f"quads_out{c}") for c in range(4)]
        codes = new([P, U], U32, "codes")
        bytes_out = new([P, U], U8, "bytes_out")

        def write_gate(t):
            nc.scalar.activation(sg[t][:], win[t][:].indirect(n3_sb[:]), SIGMOID, bias=bias[:, t : t + 1], scale=sl_sb[:, t : t + 1])

        def diff(t):
            nc.vector.tensor_tensor(step[t][:], h_ps[t][:], old[t], SUB)

        def gated(t):
            nc.vector.tensor_tensor(move[t][:], sg[t][:], step[t][:], MULT)

        def put_on_vector(t):
            nc.vector.tensor_tensor(page[t][:].indirect(n2_sb[:]), move[t][:], old[t], ADD)
            nc.sync.dma_start(out_rows[:, t, :], page[t][:])

        def add_old(t):
            nc.vector.tensor_tensor(step[t][:], move[t][:], old[t], ADD)

        def put_on_scalar(t):
            nc.scalar.activation(page[t][:].indirect(n2_sb[:]), step[t][:], COPY)
            nc.sync.dma_start(out_rows[:, t, :], page[t][:])

        def round_page(t, c):
            nc.vector.tensor_copy(pairs[c][:, t // 2, :, t % 2], page[t][:, U // 2 * c : U // 2 * (c + 1)])

        def weave(c, on_scalar):
            src = pairs[c // 2][:].rearrange("p a u b -> p (a u b)")
            dst = quads_out[c][:].rearrange("p u t -> p (u t)")
            cols = slice(U // 4 * (c % 2), U // 4 * (c % 2 + 1))
            if on_scalar:
                nc.scalar.copy(dst.bitcast(U32).rearrange("p (u a) -> p u a", a=2), src.bitcast(U32).rearrange("p (a u) -> p u a", a=2)[:, cols, :])
            else:
                nc.vector.tensor_copy(dst.bitcast(I32).rearrange("p (u a) -> p u a", a=2), src.bitcast(I32).rearrange("p (a u) -> p u a", a=2)[:, cols, :])

        words_out = out_1[0].rearrange("p u t -> p (u t)").bitcast(I32)

        def quantise_page(c):
            cols = slice(U // 4 * c, U // 4 * (c + 1))
            nc.vector.quantize_mx(out=codes[:, cols].bitcast(FP8X4), scales=bytes_out[:, cols], in_=quads_out[c][:].rearrange("p u t -> p (u t)"))

        def store_words(c0, c1):
            cols = slice(U // 4 * c0, U // 4 * c1)
            nc.sync.dma_start(words_out[:, cols], codes[:].bitcast(I32)[:, cols])

        leave_bank(h_ps[0], 0, True)
        leave_bank(h_ps[1], 1, True)
        leave_bank(h_ps[2], 2, False)
        leave_bank(h_ps[3], 3, False)
        for t in range(PACK):
            write_gate(t)
        diff(0)
        gated(0)
        diff(1)
        add_old(0)
        put_on_scalar(0)
        diff(2)
        gated(1)
        gated(2)
        diff(3)
        add_old(2)
        put_on_scalar(2)
        gated(3)
        add_old(3)
        put_on_scalar(3)
        put_on_vector(1)
        for t in (0, 2, 1, 3):
            round_page(t, 0)
            round_page(t, 1)
        weave(0, True)
        weave(1, True)
        weave(2, False)
        weave(3, True)
        quantise_page(0)
        quantise_page(2)
        quantise_page(1)
        store_words(0, 3)
        quantise_page(3)
        store_words(3, 4)

        for q in range(4):
            queue = nc.scalar if q % 2 == 0 else nc.sync
            queue.dma_start(out_2[0].bitcast(I32)[4 * q : 4 * q + 4, :], bytes_out[:].bitcast(I32)[32 * q : 32 * q + 4, :])
